import numpy as np, ml_dtypes
CORES = [36,164,52,180,100,228,116,244]
N = 8
import mx_ref
BF = ml_dtypes.bfloat16
def entries(a):
    return np.ascontiguousarray(a.T).reshape(-1)
def table(e):
    return np.ascontiguousarray(np.reshape(e, (-1, 16)).T).astype(np.int32)
def pick(q, e):
    c = np.concatenate([q[0].reshape(128, -1, 4), np.zeros((128, 1, 4), np.uint8)], axis=1); s = np.concatenate([q[1], np.ones((16, 1), np.uint8)], axis=1)
    return (np.ascontiguousarray(c[:, e].reshape(128, -1)), np.ascontiguousarray(s[:, e]))
def join(*qs):
    return (np.concatenate([q[0] for q in qs], axis=1), np.concatenate([q[1] for q in qs], axis=1))
def put(q, e, v):
    c, s = q[0].reshape(128, -1, 4).copy(), q[1].copy(); c[:, e] = v[0].reshape(128, -1, 4); s[:, e] = v[1]
    return (c.reshape(128, -1), s)
def pk(c, s):
    return (np.ascontiguousarray(c), mx_ref.live(s))
def emit(q):
    return q[0], q[1]
def packed(v, rng):
    q = [mx_ref.quantize(np.ascontiguousarray(v[r])) for r in range(N)]
    return np.stack([a for a, b in q]), np.stack([mx_ref.plane(b, rng) for a, b in q])
def decode(q):
    o = []
    for b in range(4):
        e = np.zeros((128, 128, 4), np.float32); e[np.arange(128), np.arange(128), b] = 1
        o.append(mx_ref.matmul(mx_ref.quantize(e.reshape(128, 512).astype(BF)), q))
    return np.stack(o, axis=2).reshape(128, -1)
def f(rng, *shape):
    return mx_ref.flush((rng.standard_normal(shape, dtype=np.float32) * np.exp2(rng.integers(-2, 3, shape[:-1] + (1,)))).astype(BF))
def wide(rng, *shape, cols=0):
    v = rng.standard_normal(shape, dtype=np.float32) * np.exp2(rng.integers(-12, 13, shape)).astype(np.float32)
    if cols: v *= np.repeat(np.exp2(rng.integers(-cols, cols + 1, shape[:-2] + (1, shape[-1] // 4))) * (rng.random(shape[:-2] + (1, shape[-1] // 4)) > 0.0625), 4, axis=-1).astype(np.float32)
    return mx_ref.flush(v.astype(BF))
C, S, CAPP = 512, 256, 48
def big(v, k):
    v = v.astype(np.float32) * np.float32(k)
    v[np.abs(v) < np.float32(2.0 ** -16)] = 0
    return v.astype(BF)
def names(rng, n, each):
    out, at, m = [None] * N, 0, int(n.sum())
    if not each:
        left = np.full(C, 2)
        for s in rng.permutation(N):
            out[s] = rng.permutation(np.flatnonzero(left))[:n[s]]; left[out[s]] -= 1
        return out
    a = rng.permutation(C)[:m // each]
    if each == 2: a = np.concatenate([a, rng.permutation(a)])
    for s in rng.permutation(N):
        out[s] = a[at:at + n[s]]; at += n[s]
    return out
def lists(rng, each=0, full=False, gaps=False, silent=False):
    sn, tc = np.full((N, N * CAPP), -1), np.full((N, N * CAPP), -1)
    n = np.full((N, N), CAPP) if full else rng.integers(CAPP // 4, CAPP, (N, N))
    if gaps: n[:] = CAPP - CAPP // 6
    if silent: n[:, int(rng.integers(0, N))] = 0
    for q in range(N):
        t = names(rng, n[:, q], each)
        for s in range(N): tc[q, s * CAPP + rng.permutation(CAPP)[:n[s, q]]] = t[s]
    for s in range(N):
        used = np.concatenate([tc[q, s * CAPP:s * CAPP + CAPP] >= 0 for q in range(N)])
        e = np.concatenate([rng.permutation(S), rng.integers(0, S, N * CAPP)])[:used.sum()]
        sn[s, used] = rng.permutation(e)
    return {"sn": np.stack([table(v) for v in sn]), "tc": np.stack([table(v) for v in tc])}
def setup_inputs(rng):
    c, p = packed(big(f(rng, N, 128, 4 * C), 1), rng)
    return {"wc": c, "ws": p, "gr": big(f(rng, N, 128, 4 * S), 8), **lists(rng)}
def setup_inputs_cancel(rng):
    tc, P = lists(rng, each=2, full=True, gaps=True)["tc"], S // 2
    x = rng.integers(4, 8, (128, P, 4)) * np.exp2(rng.integers(-2, 1, (128, P, 4))) * rng.choice([-1.0, 1.0], (128, P, 4)) * np.exp2(rng.integers(-2, 3, (128, P, 1)))
    h = rng.integers(0, P, (N, C))
    c, p = packed(np.stack([x[:, h[q]].reshape(128, -1) for q in range(N)]).astype(np.float32).astype(BF), rng)
    g, sn = np.zeros((N, 128, S, 4), np.float32), np.full((N, N * CAPP), -1)
    at = np.stack([rng.permutation(S) for s in range(N)])
    for s in range(N):
        g[s][:, at[s, :P]] = 8 * x
        g[s][:, at[s, P:]] = 8 * x * np.exp2(-rng.integers(21, 25, (P, 1)))
    for q in range(N):
        t = entries(tc[q]).reshape(N, CAPP)
        o = rng.permutation(np.unique(t[t >= 0]))
        late, seen = np.zeros(C, bool), np.zeros(C, bool)
        late[o[:o.size // 2]] = True
        for s in range(N):
            k = np.flatnonzero(t[s] >= 0); e = t[s][k]
            small = seen[e] != late[e]
            sn[s, q * CAPP + k] = at[s][P * small + h[q, e]]
            seen[e] = True
    return {"wc": c, "ws": p, "gr": g.reshape(N, 128, 4 * S).astype(BF), "sn": np.stack([table(v) for v in sn]), "tc": tc}
def setup_inputs_full(rng):
    return {**setup_inputs(rng), **lists(rng, full=True)}
def setup_inputs_most(rng):
    return {**setup_inputs(rng), **lists(rng, each=1, full=True, silent=True)}
def setup_inputs_spread(rng):
    d = setup_inputs(rng)
    d["wc"], d["ws"] = packed(big(wide(rng, N, 128, 4 * C, cols=8), 1), rng)
    d["gr"] = big(wide(rng, N, 128, 4 * S, cols=8), 8)
    return d
def setup_inputs_twice(rng):
    return {**setup_inputs(rng), **lists(rng, each=2, full=True)}
def check_inputs(d):
    b = []
    for r in range(N):
        a, t = entries(d["sn"][r]), entries(d["tc"][r])
        if a.min() < -1 or a.max() >= S: b.append("sn")
        sent = np.concatenate([entries(d["sn"][s])[r * CAPP:r * CAPP + CAPP] for s in range(N)])
        bad = t.min() < -1 or t.max() >= C or ((t >= 0) != (sent >= 0)).any()
        for s in range(N):
            v = t[s * CAPP:s * CAPP + CAPP]; v = v[v >= 0]
            bad = bad or len(set(v.tolist())) != v.size
        if bad or (np.unique(t[t >= 0], return_counts=True)[1] > 2).any(): b.append("tc")
    return b
def reference(wc, ws, gr, sn, tc):
    oc, osc, up = np.zeros((N, 128, 4 * C), np.uint8), np.zeros((N, 16, C), np.uint8), np.zeros((N, 1, C), np.float32)
    g = [decode(mx_ref.quantize(np.ascontiguousarray(gr[s]))).reshape(128, S, 4) for s in range(N)]
    for q in range(N):
        w = pk(wc[q], ws[q])
        v = decode(w).reshape(128, C, 4)
        for s in range(N):
            e, t = entries(sn[s])[q * CAPP:q * CAPP + CAPP], entries(tc[q])[s * CAPP:s * CAPP + CAPP]
            k = t >= 0
            v[:, t[k]] = v[:, t[k]] - g[s][:, e[k]] * np.float32(0.125)
            up[q, 0, t[k]] += 1
        named = np.flatnonzero(up[q, 0])
        new = mx_ref.quantize(np.ascontiguousarray(v.reshape(128, -1).astype(BF)))
        oc[q], osc[q] = emit(put(w, named, pick(new, named)))
    return {"oc": oc, "osc": osc, "up": up}

@@ -1,0 +1,271 @@
+from concourse.bass import DstId, RemoteDMATransfer
+from concourse.mybir import dt, AluOpType as op, ActivationFunctionType
+
+X4, U8 = "float8_e4m3fn_x4", "uint8"
+C, S, CAPP, N = 512, 256, 48, 8
+NS = N * CAPP
+HALF = NS // 2
+ZC = 128
+NP = NS - CAPP
+FW = 672
+
+SCRATCH = {
+    "grt": ("sbuf", [128, 4 * S], "bfloat16"),
+    "sni": ("sbuf", [128, NS // 16], "int32"), "tci": ("sbuf", [128, NS // 16], "int32"),
+    "soff": ("sbuf", [128, NS // 16], "uint16"), "woff": ("sbuf", [128, NS // 16], "uint16"),
+    "gq": ("sbuf", [128, S], X4), "gqs": ("sbuf", [128, S], U8),
+    "gp": ("sbuf", [128, NS], X4), "gps": ("sbuf", [128, NS], U8),
+    "land": ("sbuf", [128, ZC + NS], X4), "lands": ("sbuf", [128, ZC + NS], U8),
+    "w2": ("sbuf", [128, C], X4), "w2s": ("sbuf", [128, C], U8),
+    "wsl": ("sbuf", [128, NS], X4), "wsls": ("sbuf", [128, NS], U8),
+    "pk": ("sbuf", [128, NS], X4), "pks": ("sbuf", [128, NS], U8),
+    "wn": ("sbuf", [128, C + NS], X4), "wns": ("sbuf", [128, C + NS], U8),
+    "on": ("sbuf", [128, C], X4), "ons": ("sbuf", [128, C], U8),
+    "zer": ("sbuf", [128, 516], "bfloat16"), "eb": ("sbuf", [128, 516], "bfloat16"), "e2": ("sbuf", [128, 516], "bfloat16"),
+    "q1": ("sbuf", [128, 512], X4), "q1s": ("sbuf", [128, 512], U8),
+    "q2": ("sbuf", [128, 512], X4), "q2s": ("sbuf", [128, 512], U8),
+    "k1": ("sbuf", [128, NS // 16], "int32"), "neg": ("sbuf", [128, NS // 16], "int32"),
+    "t2": ("sbuf", [128, NS // 16], "int32"), "t3": ("sbuf", [128, NS // 16], "int32"),
+    "toff": ("sbuf", [128, 4 * N], "uint16"),
+    "pi": ("sbuf", [128, 1], "int32"), "pm": ("sbuf", [128, 1], "int32"), "pf": ("sbuf", [128, 1], "int32"),
+    "mo": ("sbuf", [128, 1], "float32"), "me": ("sbuf", [128, 1], "float32"), "p15": ("sbuf", [128, 1], "float32"),
+    "jm": ("sbuf", [128, 32], "float32"), "jw": ("sbuf", [128, 32], "float32"),
+    "vals": ("sbuf", [128, NS], "float32"),
+    "fb": ("sbuf", [128, 16 + FW], "float32"),
+    "vv": ("sbuf", [128, 416], "bfloat16"),
+    "va": ("sbuf", [128, 352], "bfloat16"), "vb": ("sbuf", [128, 352], "bfloat16"),
+    "x0": ("sbuf", [128, 16], "float32"), "x1": ("sbuf", [128, 16], "float32"), "x2": ("sbuf", [128, 16], "float32"), "x3": ("sbuf", [128, 16], "float32"),
+    "xs": ("sbuf", [128, 24], "float32"), "poff": ("sbuf", [128, 24], "uint16"),
+    "fa": ("sbuf", [128, 512], "float32"), "fc": ("sbuf", [128, 544], "float32"),
+    "y0": ("sbuf", [128, 16], "float32"), "y1": ("sbuf", [128, 16], "float32"), "y2": ("sbuf", [128, 16], "float32"), "y3": ("sbuf", [128, 16], "float32"),
+    "ys": ("sbuf", [128, 32], "float32"), "ym": ("sbuf", [128, 32], "float32"), "foff": ("sbuf", [128, 32], "uint16"),
+    "hp": ("sbuf", [128, C + NS], "bfloat16"), "upb": ("sbuf", [128, C], "float32"),
+    "h": ("sbuf", [128, 4 * NS], "bfloat16"),
+    "psa": ("psum", [128, 2048], "float32"), "psb": ("psum", [128, 2048], "float32"),
+}
+SEMAPHORES = ["ldg", "lds", "ldt", "ldw", "ldn", "own", "st", "arr", "sent", "v", "z", "ea", "gi", "eq", "soffr", "gqr", "gpc", "gpp",
+              "woffr", "wpc", "wps", "poffr", "foffr", "hpr", "upr", "ons0", "ons1", "onc0", "onc1"] + \
+             [k + h for k in ("pc", "pp", "hs", "qn") for h in "ab"] + ["t%s%d" % (h, b) for h in "ab" for b in range(4)]
+
+
+def rank_program(g, core, T, topo):
+    rank = T.rank_of(core)
+    if rank is None:
+        return
+    V, P, A, Y = g.vector, g.tensor, g.scalar, g.sync
+    COPY = ActivationFunctionType.Copy
+    total, seen, mine = {}, {}, {}
+
+    def inc(ins, name, n=1):
+        ins.then_inc(T.sem[name], n)
+        total[name] = total.get(name, 0) + n
+        return name
+
+    def wait(qn, q, *evs):
+        for name in evs:
+            if seen.get((qn, name), 0) < total[name]:
+                q.wait_ge(T.sem[name], total[name])
+                seen[(qn, name)] = total[name]
+
+    def vi(ins, name="v"):
+        mine[inc(ins, name)] = 1
+
+    def vdep():
+        wait("v", V, *sorted(mine))
+        mine.clear()
+
+    def u8(v):
+        return v.bitcast(dt.uint8)
+
+    def u32(v):
+        return v.bitcast(dt.uint32)
+
+    inc(Y.dma_start(T.grt[:, 0:2 * S], T.gr[:, 0:2 * S]), "ldg", 16)
+    inc(A.dma_start(T.grt[:, 2 * S:4 * S], T.gr[:, 2 * S:4 * S]), "ldg", 16)
+    for k in range(8):
+        inc((Y, A)[k % 2].dma_start(T.sni[16 * k:16 * k + 16, :], T.sn[:]), "lds", 16)
+    for k in range(8):
+        inc((Y, A)[k % 2].dma_start(T.tci[16 * k:16 * k + 16, :], T.tc[:]), "ldt", 16)
+    inc(Y.dma_start(u8(T.w2[:]), T.wc[:]), "ldw", 16)
+    inc(A.dma_start(T.w2s[:], T.ws[:]), "ldw", 16)
+
+    vi(V.memset(T.zer[:], 0.0), "z")
+    wait("g", g, "z")
+    inc(g.affine_select(T.eb[:], T.zer[:], [[1, 516]], op.not_equal, 1.0, -3, -4), "ea")
+    inc(g.iota(T.k1[:], [[0, N], [16, 3]], 513, 1), "gi")
+    inc(g.iota(T.pi[:], [[1, 1]], 0, 1), "gi")
+    inc(g.iota(T.jm[:], [[16, 32]], 0, 0, allow_small_or_imprecise_dtypes=True), "gi")
+    inc(g.iota(T.vals[:], [[1, NS]], C, 0, allow_small_or_imprecise_dtypes=True), "gi")
+    vi(V.memset(T.fb[:], 0.0))
+    vi(V.memset(T.vv[:, 0:16], 0.0))
+    vi(V.memset(T.vv[:, 16 + NP:416], -200.0))
+    vi(V.memset(T.hp[:, 0:C], 0.0))
+    vdep()
+    vi(V.quantize_mx(T.land[:, 0:ZC], T.lands[:, 0:ZC], T.zer[:, 0:4 * ZC]))
+    wait("v", V, "ea")
+    vi(V.tensor_scalar(T.e2[:], T.eb[:], -0.125, None, op.mult))
+    for b in range(4):
+        vi(V.quantize_mx(T.q1[:, 128 * b:128 * b + 128], T.q1s[:, 128 * b:128 * b + 128], T.eb[:, 3 - b:515 - b]), "eq")
+    vdep()
+    for b in range(4):
+        vi(V.quantize_mx(T.q2[:, 128 * b:128 * b + 128], T.q2s[:, 128 * b:128 * b + 128], T.e2[:, 3 - b:515 - b]), "eq")
+    wait("v", V, "gi")
+    vi(V.tensor_scalar(T.pm[:], T.pi[:], 4, 1, op.logical_shift_right, op.bitwise_and))
+    vi(V.tensor_scalar(T.pf[:], T.pi[:], 15, None, op.bitwise_and))
+    vdep()
+    vi(V.tensor_copy(T.mo[:], T.pm[:]))
+    vi(V.tensor_copy(T.p15[:], T.pf[:]))
+    vdep()
+    vi(V.tensor_scalar(T.me[:], T.mo[:], -1.0, 1.0, op.mult, op.add))
+    vi(V.tensor_scalar(T.jw[:], T.jm[:], T.p15[:, 0:1], None, op.add))
+
+    wait("v", V, "lds")
+    vi(V.tensor_copy(T.soff[:], T.sni[:]), "soffr")
+    wait("v", V, "ldg")
+    vi(V.quantize_mx(T.gq[:], T.gqs[:], T.grt[:]), "gqr")
+    vdep()
+    vi(V.tensor_copy(u32(T.gp[:, 0:NS]), u32(T.gq[:, 0:S]).indirect(T.soff[:, 0:NS // 16])), "gpc")
+    wait("a", A, "soffr", "gqr")
+    inc(A.activation(T.gps[:, 0:NS], T.gqs[:, 0:S].indirect(T.soff[:, 0:NS // 16]), COPY), "gpp")
+
+    dests = [(rank + k) % N for k in range(1, N)]
+    lo = ZC + CAPP * rank
+
+    def transfers(scales):
+        out = []
+        for k, q in enumerate(dests):
+            d = T.cores[q]
+            rid, pid = topo.addr(d, core)
+            a = CAPP * q
+            src = T.gps[:, a:a + CAPP] if scales else u8(T.gp[:, a:a + CAPP])
+            dst = T.lands[:, lo:lo + CAPP] if scales else u8(T.land[:, lo:lo + CAPP])
+            out.append(RemoteDMATransfer(dst_ids=[DstId(rid=rid, pnc=pid)], dma_engine_mask=1 << topo.engines(core, d)[k],
+                                         remote_sem=T.sem.arr, src=src, dst=dst))
+        return out
+
+    wait("g", g, "gpc")
+    g.remote_dma_fused(transfers(False), local_sem=T.sem.sent)
+    wait("g", g, "gpp")
+    g.remote_dma_fused(transfers(True), local_sem=T.sem.sent)
+    total["sent"] = 2 * len(dests)
+    total["arr"] = 2 * len(dests)
+    a = CAPP * rank
+    wait("y", Y, "gpc", "gpp")
+    inc(Y.dma_start(u8(T.land[:, lo:lo + CAPP]), u8(T.gp[:, a:a + CAPP])), "own", 16)
+    inc(Y.dma_start(T.lands[:, lo:lo + CAPP], T.gps[:, a:a + CAPP]), "own", 16)
+    wait("y", Y, "sent")
+    inc(Y.dma_start(u8(T.wn[:, 0:C]), T.wc[:]), "ldn", 16)
+    inc(Y.dma_start(T.wns[:, 0:C], T.ws[:]), "ldn", 16)
+
+    wait("v", V, "ldt")
+    vi(V.tensor_copy(T.woff[:], T.tci[:]), "woffr")
+    vi(V.tensor_scalar(T.neg[:], T.tci[:], 0, None, op.is_lt))
+    vdep()
+    vi(V.tensor_tensor(T.t2[:], T.neg[:], T.k1[:], op.mult))
+    wait("v", V, "ldw")
+    vi(V.tensor_copy(u32(T.wsl[:, 0:NS]), u32(T.w2[:, 0:C]).indirect(T.woff[:, 0:NS // 16])), "wpc")
+    wait("a", A, "woffr", "ldw")
+    inc(A.activation(T.wsls[:, 0:NS], T.w2s[:, 0:C].indirect(T.woff[:, 0:NS // 16]), COPY), "wps")
+    vdep()
+    vi(V.tensor_tensor(T.t3[:], T.tci[:], T.t2[:], op.add))
+    vdep()
+    for i in range(3):
+        vi(V.tensor_copy(T.toff[:, i:4 * N:4], T.t3[:, i:NS // 16:3]))
+    for s in range(N - 1, -1, -1):
+        off = T.toff[:, 4 * s:4 * s + 3]
+        e = CAPP * s
+        vdep()
+        if s < N - 1:
+            vi(V.tensor_scalar(T.vv[:, 16 + e:16 + e + CAPP], T.fb[:, 16:16 + FW].indirect(off), -704.0, -200.0, op.add, op.max))
+            vdep()
+        vi(V.tensor_copy(T.fb[:, 16:16 + FW].indirect(off), T.vals[:, e:e + CAPP]))
+    vdep()
+    vi(V.transpose(T.va[:], T.vv[:, 16:368]))
+    vi(V.transpose(T.vb[:], T.vv[:, 0:352]))
+    vi(V.tensor_scalar(T.hp[:, C:C + NS], T.vv[:, 16:16 + NS], -192.0, 1.0, op.is_ge, op.add), "hpr")
+    vdep()
+    vi(V.tensor_scalar(T.x0[:, 0:11], T.va[:, 0:352:32], T.me[:, 0:1], None, op.mult))
+    vi(V.tensor_scalar(T.x1[:, 0:11], T.vb[:, 0:352:32], T.mo[:, 0:1], None, op.mult))
+    vi(V.tensor_scalar(T.x2[:, 0:10], T.va[:, 0:320:32], T.mo[:, 0:1], None, op.mult))
+    vi(V.tensor_scalar(T.x3[:, 0:10], T.vb[:, 32:352:32], T.me[:, 0:1], None, op.mult))
+    vdep()
+    vi(V.tensor_tensor(T.xs[:, 0:21:2], T.x0[:, 0:11], T.x1[:, 0:11], op.add))
+    vi(V.tensor_tensor(T.xs[:, 1:21:2], T.x2[:, 0:10], T.x3[:, 0:10], op.add))
+    vdep()
+    vi(V.tensor_scalar(T.poff[:, 0:21], T.xs[:, 0:21], 192.0 + ZC, None, op.add), "poffr")
+    vi(V.transpose(T.fa[:], T.fb[:, 16:528]))
+    vi(V.transpose(T.fc[:], T.fb[:, 0:544]))
+    vdep()
+    vi(V.tensor_scalar(T.y0[:], T.fa[:, 0:512:32], T.me[:, 0:1], None, op.mult))
+    vi(V.tensor_scalar(T.y1[:], T.fc[:, 0:512:32], T.mo[:, 0:1], None, op.mult))
+    vi(V.tensor_scalar(T.y2[:], T.fa[:, 0:512:32], T.mo[:, 0:1], None, op.mult))
+    vi(V.tensor_scalar(T.y3[:], T.fc[:, 32:544:32], T.me[:, 0:1], None, op.mult))
+    vdep()
+    vi(V.tensor_tensor(T.ys[:, 0:32:2], T.y0[:], T.y1[:], op.add))
+    vi(V.tensor_tensor(T.ys[:, 1:32:2], T.y2[:], T.y3[:], op.add))
+    vdep()
+    vi(V.tensor_tensor(T.ym[:], T.ys[:], T.jw[:], op.max))
+    vdep()
+    vi(V.tensor_copy(T.foff[:], T.ym[:]), "foffr")
+
+    halves = (("a", T.psa, 0, HALF, HALF), ("b", T.psb, HALF, HALF, NP - HALF))
+
+    def product(ps, b, n, e, es, x, xs, at, start, stop):
+        return P.matmul_mx(ps[:, 512 * b:512 * b + n], e[:, 128 * b:128 * b + 128], es[:, 128 * b:128 * b + 128],
+                           x[:, at:at + n], xs[:, at:at + n], start, stop)
+
+    wait("p", P, "eq", "wpc", "wps")
+    for name, ps, at, n, m in halves:
+        for b in range(4):
+            product(ps, b, n, T.q1, T.q1s, T.wsl, T.wsls, at, True, False)
+    wait("p", P, "arr", "own")
+    wait("v", V, "arr", "own")
+    wait("a", A, "arr", "own", "poffr")
+    vdep()
+    for name, ps, at, n, m in halves:
+        off = T.poff[:, at // 16:(at + m) // 16]
+        vi(V.tensor_copy(u32(T.pk[:, at:at + m]), u32(T.land[:, 0:ZC + NS]).indirect(off)), "pc" + name)
+        inc(A.activation(T.pks[:, at:at + m], T.lands[:, 0:ZC + NS].indirect(off), COPY), "pp" + name)
+    for name, ps, at, n, m in halves:
+        for b in range(4):
+            product(ps, b, n, T.q2, T.q2s, T.land, T.lands, ZC + at, False, False)
+        wait("p", P, "pc" + name, "pp" + name)
+        for b in range(4):
+            inc(product(ps, b, m, T.q2, T.q2s, T.pk, T.pks, at, False, True), "t%s%d" % (name, b))
+    wait("a", A, "foffr", "hpr")
+    inc(A.activation(T.upb[:], T.hp[:, 0:C + NS].indirect(T.foff[:, 0:32]), COPY), "upr")
+
+    for name, ps, at, n, m in halves:
+        for b in range(4):
+            out, src = T.h[:, 4 * at + b:4 * (at + n):4], ps[:, 512 * b:512 * b + n]
+            if b % 2 == 0:
+                wait("v", V, "t%s%d" % (name, b))
+                vi(V.tensor_copy(out, src))
+            else:
+                wait("a", A, "t%s%d" % (name, b))
+                inc(A.activation(out, src, COPY), "hs" + name)
+        wait("v", V, "hs" + name)
+        vdep()
+        vi(V.quantize_mx(T.wn[:, C + at:C + at + n], T.wns[:, C + at:C + at + n], T.h[:, 4 * at:4 * (at + n)]), "qn" + name)
+
+    wait("v", V, "ldn")
+    vdep()
+    wait("a", A, "ldn", "qna", "qnb")
+    for k in range(2):
+        off = T.foff[:, 16 * k:16 * k + 16]
+        vi(V.tensor_copy(u32(T.on[:, 256 * k:256 * k + 256]), u32(T.wn[:, 0:C + NS]).indirect(off)), "onc%d" % k)
+        inc(A.activation(T.ons[:, 256 * k:256 * k + 256], T.wns[:, 0:C + NS].indirect(off), COPY), "ons%d" % k)
+    wait("y", Y, "upr")
+    inc(Y.dma_start(T.up[:], T.upb[0:1, :]), "st", 16)
+    for k in range(2):
+        wait("y", Y, "onc%d" % k)
+        inc(Y.dma_start(T.oc[:, 1024 * k:1024 * k + 1024], u8(T.on[:, 256 * k:256 * k + 256])), "st", 16)
+    for k in range(4):
+        qn, q = (("a", A), ("y", Y))[k // 2]
+        wait(qn, q, "ons0", "ons1")
+        inc(q.dma_start(T.osc[4 * k:4 * k + 4, :], T.ons[32 * k:32 * k + 4, :]), "st", 16)
+
+    for name in total:
+        if name not in ("st",):
+            wait("g", g, name)
+    wait("y", Y, "st")

@@ -8,6 +8,8 @@ HALF = NS // 2
 ZC = 128
 NP = NS - CAPP
 FW = 672
+MID, NONE = 192.0, -768.0
+TO = C + MID
 
 SCRATCH = {
     "grt": ("sbuf", [128, 4 * S], "bfloat16"),
@@ -26,25 +28,28 @@ SCRATCH = {
     "q2": ("sbuf", [128, 512], X4), "q2s": ("sbuf", [128, 512], U8),
     "k1": ("sbuf", [128, NS // 16], "int32"), "neg": ("sbuf", [128, NS // 16], "int32"),
     "t2": ("sbuf", [128, NS // 16], "int32"), "t3": ("sbuf", [128, NS // 16], "int32"),
-    "toff": ("sbuf", [128, 4 * N], "uint16"),
-    "pi": ("sbuf", [128, 1], "int32"), "pm": ("sbuf", [128, 1], "int32"), "pf": ("sbuf", [128, 1], "int32"),
-    "mo": ("sbuf", [128, 1], "float32"), "me": ("sbuf", [128, 1], "float32"), "p15": ("sbuf", [128, 1], "float32"),
-    "jm": ("sbuf", [128, 32], "float32"), "jw": ("sbuf", [128, 32], "float32"),
-    "vals": ("sbuf", [128, NS], "float32"),
-    "fb": ("sbuf", [128, 16 + FW], "float32"),
+    "toff": ("sbuf", [128, NS // 16], "uint16"), "tord": ("sbuf", [128, 4 * N], "uint16"), "coff": ("sbuf", [128, 2], "uint16"),
+    "pi": ("sbuf", [128, 1], "int32"), "c48": ("sbuf", [128, CAPP], "float32"), "i8": ("sbuf", [128, N], "float32"), "colv": ("sbuf", [128, N], "float32"),
+    "jm": ("sbuf", [128, 32], "float32"), "jw": ("sbuf", [128, 32], "float32"), "ew": ("sbuf", [128, 32], "float32"),
+    "vals": ("sbuf", [128, NS], "bfloat16"),
+    "fb": ("sbuf", [128, 16 + FW], "bfloat16"),
     "vv": ("sbuf", [128, 416], "bfloat16"),
     "va": ("sbuf", [128, 352], "bfloat16"), "vb": ("sbuf", [128, 352], "bfloat16"),
-    "x0": ("sbuf", [128, 16], "float32"), "x1": ("sbuf", [128, 16], "float32"), "x2": ("sbuf", [128, 16], "float32"), "x3": ("sbuf", [128, 16], "float32"),
-    "xs": ("sbuf", [128, 24], "float32"), "poff": ("sbuf", [128, 24], "uint16"),
-    "fa": ("sbuf", [128, 512], "float32"), "fc": ("sbuf", [128, 544], "float32"),
-    "y0": ("sbuf", [128, 16], "float32"), "y1": ("sbuf", [128, 16], "float32"), "y2": ("sbuf", [128, 16], "float32"), "y3": ("sbuf", [128, 16], "float32"),
+    "xs": ("sbuf", [128, 24], "float32"), "xn": ("sbuf", [128, 24], "float32"), "xm": ("sbuf", [128, 24], "float32"), "poff": ("sbuf", [128, 24], "uint16"),
+    "fa": ("sbuf", [128, 512], "bfloat16"), "fc": ("sbuf", [128, 544], "bfloat16"),
     "ys": ("sbuf", [128, 32], "float32"), "ym": ("sbuf", [128, 32], "float32"), "foff": ("sbuf", [128, 32], "uint16"),
-    "hp": ("sbuf", [128, C + NS], "bfloat16"), "upb": ("sbuf", [128, C], "float32"),
+    "ub": ("sbuf", [128, 32], "float32"), "ut": ("sbuf", [128, 32], "float32"),
     "h": ("sbuf", [128, 4 * NS], "bfloat16"),
     "psa": ("psum", [128, 2048], "float32"), "psb": ("psum", [128, 2048], "float32"),
 }
-SEMAPHORES = ["ldg", "lds", "ldt", "ldw", "ldn", "own", "st", "arr", "sent", "v", "z", "ea", "gi", "eq", "soffr", "gqr", "gpc", "gpp",
-              "woffr", "wpc", "wps", "poffr", "foffr", "hpr", "upr", "ons0", "ons1", "onc0", "onc1"] + \
+for _k in ("pm", "p15i", "p4i", "p3i"):
+    SCRATCH[_k] = ("sbuf", [128, 1], "int32")
+for _k in ("mo", "me", "p15", "p4", "p3", "sg", "cm", "ca", "cb", "cd"):
+    SCRATCH[_k] = ("sbuf", [128, 1], "float32")
+for _k in ("x0", "x1", "x2", "x3", "y0", "y1", "y2", "y3", "u0", "u1"):
+    SCRATCH[_k] = ("sbuf", [128, 16], "float32")
+SEMAPHORES = ["ldg", "lds", "ldt", "ldw", "ldn", "own", "st", "arr", "sent", "v", "z", "ea", "e2r", "gi", "eq", "cv", "vl", "soffr", "gqr", "gpc", "gpp",
+              "woffr", "tof", "fg", "vg", "wpc", "wps", "poffr", "foffr", "utr", "ons0", "ons1", "onc0", "onc1"] + \
              [k + h for k in ("pc", "pp", "hs", "qn") for h in "ab"] + ["t%s%d" % (h, b) for h in "ab" for b in range(4)]
 
 
@@ -53,7 +58,7 @@ def rank_program(g, core, T, topo):
     if rank is None:
         return
     V, P, A, Y = g.vector, g.tensor, g.scalar, g.sync
-    COPY = ActivationFunctionType.Copy
+    COPY, IDENT = ActivationFunctionType.Copy, ActivationFunctionType.Identity
     total, seen, mine = {}, {}, {}
 
     def inc(ins, name, n=1):
@@ -80,6 +85,17 @@ def rank_program(g, core, T, topo):
     def u32(v):
         return v.bitcast(dt.uint32)
 
+    def choose(out, n, even, odd, ins, add):
+        (a0, b0), (a1, b1) = even, odd
+        ne, no = (n + 1) // 2, n // 2
+        for x, v, m in ((ins[0], a0, T.me), (ins[1], b0, T.mo), (ins[2], a1, T.me), (ins[3], b1, T.mo)):
+            k = ne if x in ins[:2] else no
+            vi(V.tensor_scalar(T[x][:, 0:k], v, add, m[:, 0:1], op.add, op.mult))
+        vdep()
+        vi(V.tensor_tensor(out[:, 0:n:2], T[ins[0]][:, 0:ne], T[ins[1]][:, 0:ne], op.add))
+        vi(V.tensor_tensor(out[:, 1:n:2], T[ins[2]][:, 0:no], T[ins[3]][:, 0:no], op.add))
+        vdep()
+
     inc(Y.dma_start(T.grt[:, 0:2 * S], T.gr[:, 0:2 * S]), "ldg", 16)
     inc(A.dma_start(T.grt[:, 2 * S:4 * S], T.gr[:, 2 * S:4 * S]), "ldg", 16)
     for k in range(8):
@@ -90,37 +106,70 @@ def rank_program(g, core, T, topo):
     inc(A.dma_start(T.w2s[:], T.ws[:]), "ldw", 16)
 
     vi(V.memset(T.zer[:], 0.0), "z")
+    F32 = {"allow_small_or_imprecise_dtypes": True}
+    inc(g.iota(T.pi[:], [[1, 1]], 0, 1), "gi")
+    inc(g.iota(T.jm[:], [[16, 32]], 0, 0, **F32), "gi")
+    inc(g.iota(T.i8[:], [[CAPP, N]], -168, 0, **F32), "gi")
+    inc(g.iota(T.c48[:], [[1, CAPP]], 0, 0, **F32), "gi")
+    inc(g.iota(T.k1[:], [[0, N], [16, 3]], C + 1, 1), "gi")
     wait("g", g, "z")
     inc(g.affine_select(T.eb[:], T.zer[:], [[1, 516]], op.not_equal, 1.0, -3, -4), "ea")
-    inc(g.iota(T.k1[:], [[0, N], [16, 3]], 513, 1), "gi")
-    inc(g.iota(T.pi[:], [[1, 1]], 0, 1), "gi")
-    inc(g.iota(T.jm[:], [[16, 32]], 0, 0, allow_small_or_imprecise_dtypes=True), "gi")
-    inc(g.iota(T.vals[:], [[1, NS]], C, 0, allow_small_or_imprecise_dtypes=True), "gi")
-    vi(V.memset(T.fb[:], 0.0))
+    vi(V.memset(T.fb[:], NONE))
     vi(V.memset(T.vv[:, 0:16], 0.0))
-    vi(V.memset(T.vv[:, 16 + NP:416], -200.0))
-    vi(V.memset(T.hp[:, 0:C], 0.0))
-    vdep()
-    vi(V.quantize_mx(T.land[:, 0:ZC], T.lands[:, 0:ZC], T.zer[:, 0:4 * ZC]))
-    wait("v", V, "ea")
-    vi(V.tensor_scalar(T.e2[:], T.eb[:], -0.125, None, op.mult))
-    for b in range(4):
-        vi(V.quantize_mx(T.q1[:, 128 * b:128 * b + 128], T.q1s[:, 128 * b:128 * b + 128], T.eb[:, 3 - b:515 - b]), "eq")
-    vdep()
-    for b in range(4):
-        vi(V.quantize_mx(T.q2[:, 128 * b:128 * b + 128], T.q2s[:, 128 * b:128 * b + 128], T.e2[:, 3 - b:515 - b]), "eq")
+    vi(V.memset(T.vv[:, 16 + NP:416], 0.0))
+    vi(V.memset(T.ub[:], 0.0))
     wait("v", V, "gi")
     vi(V.tensor_scalar(T.pm[:], T.pi[:], 4, 1, op.logical_shift_right, op.bitwise_and))
-    vi(V.tensor_scalar(T.pf[:], T.pi[:], 15, None, op.bitwise_and))
+    vi(V.tensor_scalar(T.p15i[:], T.pi[:], 15, None, op.bitwise_and))
+    vi(V.tensor_scalar(T.p4i[:], T.pi[:], 2, 3, op.logical_shift_right, op.bitwise_and))
+    vi(V.tensor_scalar(T.p3i[:], T.pi[:], 3, None, op.bitwise_and))
     vdep()
     vi(V.tensor_copy(T.mo[:], T.pm[:]))
-    vi(V.tensor_copy(T.p15[:], T.pf[:]))
+    vi(V.tensor_copy(T.p15[:], T.p15i[:]))
+    vi(V.tensor_copy(T.p4[:], T.p4i[:]))
+    vi(V.tensor_copy(T.p3[:], T.p3i[:]))
     vdep()
+    vi(V.tensor_scalar(T.sg[:], T.mo[:], 2.0, -1.0, op.mult, op.add))
     vi(V.tensor_scalar(T.me[:], T.mo[:], -1.0, 1.0, op.mult, op.add))
-    vi(V.tensor_scalar(T.jw[:], T.jm[:], T.p15[:, 0:1], None, op.add))
+    vi(V.tensor_scalar(T.jw[:], T.jm[:], T.p15[:, 0:1], -TO, op.add, op.add))
+    vi(V.tensor_scalar(T.ew[:], T.jm[:], T.p15[:, 0:1], float(ZC), op.add, op.add))
+    vi(V.tensor_scalar(T.cm[:], T.p3[:], 2.0, None, op.min))
+    vdep()
+    vi(V.tensor_scalar(T.colv[:], T.i8[:], T.sg[:, 0:1], -24.0, op.mult, op.add), "cv")
+    vi(V.tensor_scalar(T.ca[:], T.p4[:], 3.0, T.sg[:, 0:1], op.mult, op.mult))
+    vdep()
+    vi(V.tensor_tensor(T.cb[:], T.ca[:], T.cm[:], op.add))
+    vdep()
+    vi(V.tensor_scalar(T.coff[:, 0:1], T.me[:], 21.0, T.cb[:, 0:1], op.mult, op.add))
+    vi(V.tensor_scalar(T.cd[:], T.me[:], -3.0, T.cb[:, 0:1], op.mult, op.add))
+    vdep()
+    vi(V.tensor_scalar(T.coff[:, 1:2], T.cd[:], 12.0, None, op.add))
+    wait("a", A, "ea")
+    inc(A.activation(T.e2[:], T.eb[:], COPY, scale=-0.125), "e2r")
+    wait("a", A, "cv", "gi")
+    for i in range(N):
+        inc(A.activation(T.vals[:, CAPP * i:CAPP * i + CAPP], T.c48[:], IDENT, bias=T.colv[:, i:i + 1]), "vl")
+    vi(V.quantize_mx(T.land[:, 0:ZC], T.lands[:, 0:ZC], T.zer[:, 0:4 * ZC]))
+    wait("v", V, "ea")
+    for b in range(4):
+        vi(V.quantize_mx(T.q1[:, 128 * b:128 * b + 128], T.q1s[:, 128 * b:128 * b + 128], T.eb[:, 3 - b:515 - b]), "eq")
+    wait("v", V, "e2r")
+    for b in range(4):
+        vi(V.quantize_mx(T.q2[:, 128 * b:128 * b + 128], T.q2s[:, 128 * b:128 * b + 128], T.e2[:, 3 - b:515 - b]), "eq")
 
     wait("v", V, "lds")
     vi(V.tensor_copy(T.soff[:], T.sni[:]), "soffr")
+    wait("v", V, "ldt")
+    vi(V.tensor_scalar(T.neg[:], T.tci[:], 0, None, op.is_lt))
+    vi(V.tensor_copy(T.woff[:], T.tci[:]), "woffr")
+    vdep()
+    vi(V.tensor_tensor(T.t2[:], T.neg[:], T.k1[:], op.mult))
+    vdep()
+    vi(V.tensor_tensor(T.t3[:], T.tci[:], T.t2[:], op.add))
+    vdep()
+    vi(V.tensor_copy(T.toff[:], T.t3[:]), "tof")
+    vi(V.tensor_copy(T.tord[:], T.t3[:, 0:NS // 16].indirect(T.coff[:, 0:2])))
+
     wait("v", V, "ldg")
     vi(V.quantize_mx(T.gq[:], T.gqs[:], T.grt[:]), "gqr")
     vdep()
@@ -157,56 +206,35 @@ def rank_program(g, core, T, topo):
     inc(Y.dma_start(u8(T.wn[:, 0:C]), T.wc[:]), "ldn", 16)
     inc(Y.dma_start(T.wns[:, 0:C], T.ws[:]), "ldn", 16)
 
-    wait("v", V, "ldt")
-    vi(V.tensor_copy(T.woff[:], T.tci[:]), "woffr")
-    vi(V.tensor_scalar(T.neg[:], T.tci[:], 0, None, op.is_lt))
-    vdep()
-    vi(V.tensor_tensor(T.t2[:], T.neg[:], T.k1[:], op.mult))
-    wait("v", V, "ldw")
-    vi(V.tensor_copy(u32(T.wsl[:, 0:NS]), u32(T.w2[:, 0:C]).indirect(T.woff[:, 0:NS // 16])), "wpc")
+    win = T.fb[:, 16:16 + FW]
+    wait("v", V, "vl")
+    for i in range(N):
+        vdep()
+        vi(V.tensor_copy(win.indirect(T.tord[:, 4 * i:4 * i + 3]), T.vals[:, CAPP * i:CAPP * i + CAPP]), "fg")
     wait("a", A, "woffr", "ldw")
     inc(A.activation(T.wsls[:, 0:NS], T.w2s[:, 0:C].indirect(T.woff[:, 0:NS // 16]), COPY), "wps")
-    vdep()
-    vi(V.tensor_tensor(T.t3[:], T.tci[:], T.t2[:], op.add))
-    vdep()
-    for i in range(3):
-        vi(V.tensor_copy(T.toff[:, i:4 * N:4], T.t3[:, i:NS // 16:3]))
-    for s in range(N - 1, -1, -1):
-        off = T.toff[:, 4 * s:4 * s + 3]
-        e = CAPP * s
-        vdep()
-        if s < N - 1:
-            vi(V.tensor_scalar(T.vv[:, 16 + e:16 + e + CAPP], T.fb[:, 16:16 + FW].indirect(off), -704.0, -200.0, op.add, op.max))
-            vdep()
-        vi(V.tensor_copy(T.fb[:, 16:16 + FW].indirect(off), T.vals[:, e:e + CAPP]))
+    wait("a", A, "fg", "tof")
+    inc(A.activation(T.vv[:, 16:16 + NP], win.indirect(T.toff[:, 0:NP // 16]), COPY), "vg")
+    wait("v", V, "ldw")
+    vi(V.tensor_copy(u32(T.wsl[:, 0:NS]), u32(T.w2[:, 0:C]).indirect(T.woff[:, 0:NS // 16])), "wpc")
+    wait("v", V, "vg")
     vdep()
     vi(V.transpose(T.va[:], T.vv[:, 16:368]))
     vi(V.transpose(T.vb[:], T.vv[:, 0:352]))
-    vi(V.tensor_scalar(T.hp[:, C:C + NS], T.vv[:, 16:16 + NS], -192.0, 1.0, op.is_ge, op.add), "hpr")
     vdep()
-    vi(V.tensor_scalar(T.x0[:, 0:11], T.va[:, 0:352:32], T.me[:, 0:1], None, op.mult))
-    vi(V.tensor_scalar(T.x1[:, 0:11], T.vb[:, 0:352:32], T.mo[:, 0:1], None, op.mult))
-    vi(V.tensor_scalar(T.x2[:, 0:10], T.va[:, 0:320:32], T.mo[:, 0:1], None, op.mult))
-    vi(V.tensor_scalar(T.x3[:, 0:10], T.vb[:, 32:352:32], T.me[:, 0:1], None, op.mult))
+    choose(T.xs, 21, (T.va[:, 16:352:32], T.vb[:, 16:352:32]), (T.vb[:, 48:352:32], T.va[:, 16:336:32]), ("x0", "x1", "x2", "x3"), MID + ZC)
+    vi(V.tensor_tensor(T.xn[:, 0:21], T.xs[:, 0:21], T.ew[:, 0:21], op.not_equal))
     vdep()
-    vi(V.tensor_tensor(T.xs[:, 0:21:2], T.x0[:, 0:11], T.x1[:, 0:11], op.add))
-    vi(V.tensor_tensor(T.xs[:, 1:21:2], T.x2[:, 0:10], T.x3[:, 0:10], op.add))
+    vi(V.tensor_tensor(T.xm[:, 0:21], T.xs[:, 0:21], T.xn[:, 0:21], op.mult))
     vdep()
-    vi(V.tensor_scalar(T.poff[:, 0:21], T.xs[:, 0:21], 192.0 + ZC, None, op.add), "poffr")
+    vi(V.tensor_copy(T.poff[:, 0:21], T.xm[:, 0:21]), "poffr")
     vi(V.transpose(T.fa[:], T.fb[:, 16:528]))
     vi(V.transpose(T.fc[:], T.fb[:, 0:544]))
     vdep()
-    vi(V.tensor_scalar(T.y0[:], T.fa[:, 0:512:32], T.me[:, 0:1], None, op.mult))
-    vi(V.tensor_scalar(T.y1[:], T.fc[:, 0:512:32], T.mo[:, 0:1], None, op.mult))
-    vi(V.tensor_scalar(T.y2[:], T.fa[:, 0:512:32], T.mo[:, 0:1], None, op.mult))
-    vi(V.tensor_scalar(T.y3[:], T.fc[:, 32:544:32], T.me[:, 0:1], None, op.mult))
-    vdep()
-    vi(V.tensor_tensor(T.ys[:, 0:32:2], T.y0[:], T.y1[:], op.add))
-    vi(V.tensor_tensor(T.ys[:, 1:32:2], T.y2[:], T.y3[:], op.add))
-    vdep()
+    choose(T.ys, 32, (T.fa[:, 0:512:32], T.fc[:, 0:512:32]), (T.fc[:, 32:544:32], T.fa[:, 0:512:32]), ("y0", "y1", "y2", "y3"), 0.0)
     vi(V.tensor_tensor(T.ym[:], T.ys[:], T.jw[:], op.max))
     vdep()
-    vi(V.tensor_copy(T.foff[:], T.ym[:]), "foffr")
+    vi(V.tensor_scalar(T.foff[:], T.ym[:], TO, None, op.add), "foffr")
 
     halves = (("a", T.psa, 0, HALF, HALF), ("b", T.psb, HALF, HALF, NP - HALF))
 
@@ -232,8 +260,12 @@ def rank_program(g, core, T, topo):
         wait("p", P, "pc" + name, "pp" + name)
         for b in range(4):
             inc(product(ps, b, m, T.q2, T.q2s, T.pk, T.pks, at, False, True), "t%s%d" % (name, b))
-    wait("a", A, "foffr", "hpr")
-    inc(A.activation(T.upb[:], T.hp[:, 0:C + NS].indirect(T.foff[:, 0:32]), COPY), "upr")
+    vi(V.tensor_scalar(T.u0[:], T.fa[:, 0:512:32], -MID, None, op.is_ge))
+    vi(V.tensor_tensor(T.u1[:], T.fa[:, 0:512:32], T.fa[:, 16:512:32], op.not_equal))
+    vdep()
+    vi(V.tensor_tensor(T.ub[:, 0:16], T.u0[:], T.u1[:], op.add))
+    vdep()
+    vi(V.transpose(T.ut[:], T.ub[:]), "utr")
 
     for name, ps, at, n, m in halves:
         for b in range(4):
@@ -250,13 +282,13 @@ def rank_program(g, core, T, topo):
 
     wait("v", V, "ldn")
     vdep()
-    wait("a", A, "ldn", "qna", "qnb")
+    wait("a", A, "ldn", "qna", "qnb", "foffr")
     for k in range(2):
         off = T.foff[:, 16 * k:16 * k + 16]
         vi(V.tensor_copy(u32(T.on[:, 256 * k:256 * k + 256]), u32(T.wn[:, 0:C + NS]).indirect(off)), "onc%d" % k)
         inc(A.activation(T.ons[:, 256 * k:256 * k + 256], T.wns[:, 0:C + NS].indirect(off), COPY), "ons%d" % k)
-    wait("y", Y, "upr")
-    inc(Y.dma_start(T.up[:], T.upb[0:1, :]), "st", 16)
+    wait("y", Y, "utr")
+    inc(Y.dma_start(T.up[:], T.ut[0:16, :]), "st", 16)
     for k in range(2):
         wait("y", Y, "onc%d" % k)
         inc(Y.dma_start(T.oc[:, 1024 * k:1024 * k + 1024], u8(T.on[:, 256 * k:256 * k + 256])), "st", 16)

@@ -7,49 +7,46 @@ NS = N * CAPP
 HALF = NS // 2
 ZC = 128
 NP = NS - CAPP
-FW = 672
-MID, NONE = 192.0, -768.0
-TO = C + MID
+NV = 352
+FW = C + 160
+MID, NONE = 192, 768
+LC = NS // 16
+BF_, BV = C // 32, NV // 32
+NB = BF_ + BV
 
 SCRATCH = {
     "grt": ("sbuf", [128, 4 * S], "bfloat16"),
-    "sni": ("sbuf", [128, NS // 16], "int32"), "tci": ("sbuf", [128, NS // 16], "int32"),
-    "soff": ("sbuf", [128, NS // 16], "uint16"), "woff": ("sbuf", [128, NS // 16], "uint16"),
+    "sni": ("sbuf", [128, LC], "int32"), "tci": ("sbuf", [128, 28], "int32"),
+    "soff": ("sbuf", [128, LC], "uint16"), "woff": ("sbuf", [128, LC], "uint16"),
     "gq": ("sbuf", [128, S], X4), "gqs": ("sbuf", [128, S], U8),
     "gp": ("sbuf", [128, NS], X4), "gps": ("sbuf", [128, NS], U8),
-    "land": ("sbuf", [128, ZC + NS], X4), "lands": ("sbuf", [128, ZC + NS], U8),
+    "land": ("sbuf", [128, NS + ZC], X4), "lands": ("sbuf", [128, NS + ZC], U8),
     "w2": ("sbuf", [128, C], X4), "w2s": ("sbuf", [128, C], U8),
     "wsl": ("sbuf", [128, NS], X4), "wsls": ("sbuf", [128, NS], U8),
     "pk": ("sbuf", [128, NS], X4), "pks": ("sbuf", [128, NS], U8),
-    "wn": ("sbuf", [128, C + NS], X4), "wns": ("sbuf", [128, C + NS], U8),
+    "wn": ("sbuf", [128, NS + C], X4), "wns": ("sbuf", [128, NS + C], U8),
     "on": ("sbuf", [128, C], X4), "ons": ("sbuf", [128, C], U8),
     "zer": ("sbuf", [128, 516], "bfloat16"), "eb": ("sbuf", [128, 516], "bfloat16"), "e2": ("sbuf", [128, 516], "bfloat16"),
     "q1": ("sbuf", [128, 512], X4), "q1s": ("sbuf", [128, 512], U8),
     "q2": ("sbuf", [128, 512], X4), "q2s": ("sbuf", [128, 512], U8),
-    "k1": ("sbuf", [128, NS // 16], "int32"), "neg": ("sbuf", [128, NS // 16], "int32"),
-    "t2": ("sbuf", [128, NS // 16], "int32"), "t3": ("sbuf", [128, NS // 16], "int32"),
-    "toff": ("sbuf", [128, NS // 16], "uint16"), "tord": ("sbuf", [128, 4 * N], "uint16"), "coff": ("sbuf", [128, 2], "uint16"),
-    "pi": ("sbuf", [128, 1], "int32"), "c48": ("sbuf", [128, CAPP], "float32"), "i8": ("sbuf", [128, N], "float32"), "colv": ("sbuf", [128, N], "float32"),
-    "jm": ("sbuf", [128, 32], "float32"), "jw": ("sbuf", [128, 32], "float32"), "ew": ("sbuf", [128, 32], "float32"),
-    "vals": ("sbuf", [128, NS], "bfloat16"),
-    "fb": ("sbuf", [128, 16 + FW], "bfloat16"),
-    "vv": ("sbuf", [128, 416], "bfloat16"),
-    "va": ("sbuf", [128, 352], "bfloat16"), "vb": ("sbuf", [128, 352], "bfloat16"),
-    "xs": ("sbuf", [128, 24], "float32"), "xn": ("sbuf", [128, 24], "float32"), "xm": ("sbuf", [128, 24], "float32"), "poff": ("sbuf", [128, 24], "uint16"),
-    "fa": ("sbuf", [128, 512], "bfloat16"), "fc": ("sbuf", [128, 544], "bfloat16"),
-    "ys": ("sbuf", [128, 32], "float32"), "ym": ("sbuf", [128, 32], "float32"), "foff": ("sbuf", [128, 32], "uint16"),
+    "k1": ("sbuf", [128, 28], "int32"), "t2": ("sbuf", [128, 28], "int32"), "t3": ("sbuf", [128, 28], "int32"),
+    "toff": ("sbuf", [128, 28], "uint16"),
+    "vals": ("sbuf", [128, CAPP], "bfloat16"),
+    "fb": ("sbuf", [128, FW], "bfloat16"),
+    "vv": ("sbuf", [128, NV], "bfloat16"),
+    "tt": ("sbuf", [128, C + NV], "bfloat16"),
+    "sa": ("sbuf", [128, 32], "float32"), "sb": ("sbuf", [128, 32], "float32"), "sc": ("sbuf", [128, 32], "float32"),
+    "ma": ("sbuf", [128, 16], "float32"), "mb": ("sbuf", [128, 16], "float32"), "mc": ("sbuf", [128, 16], "float32"),
+    "kf": ("sbuf", [128, 16], "float32"), "kv": ("sbuf", [128, 16], "float32"), "dv": ("sbuf", [128, 16], "float32"),
+    "r": ("sbuf", [128, 32], "float32"), "z": ("sbuf", [128, 64], "float32"), "y": ("sbuf", [128, 64], "float32"),
+    "lst": ("sbuf", [128, 64], "uint16"),
+    "u0": ("sbuf", [128, 16], "float32"), "u1": ("sbuf", [128, 16], "float32"),
     "ub": ("sbuf", [128, 32], "float32"), "ut": ("sbuf", [128, 32], "float32"),
     "h": ("sbuf", [128, 4 * NS], "bfloat16"),
     "psa": ("psum", [128, 2048], "float32"), "psb": ("psum", [128, 2048], "float32"),
 }
-for _k in ("pm", "p15i", "p4i", "p3i"):
-    SCRATCH[_k] = ("sbuf", [128, 1], "int32")
-for _k in ("mo", "me", "p15", "p4", "p3", "sg", "cm", "ca", "cb", "cd"):
-    SCRATCH[_k] = ("sbuf", [128, 1], "float32")
-for _k in ("x0", "x1", "x2", "x3", "y0", "y1", "y2", "y3", "u0", "u1"):
-    SCRATCH[_k] = ("sbuf", [128, 16], "float32")
-SEMAPHORES = ["ldg", "lds", "ldt", "ldw", "ldn", "own", "st", "arr", "sent", "v", "z", "ea", "e2r", "gi", "eq", "cv", "vl", "soffr", "gqr", "gpc", "gpp",
-              "woffr", "tof", "fg", "vg", "wpc", "wps", "poffr", "foffr", "utr", "ons0", "ons1", "onc0", "onc1"] + \
+SEMAPHORES = ["ldg", "lds", "ldt", "ldw", "ldn", "ownc", "owns", "st", "arc", "ars", "sent", "v", "z", "gi", "ea", "e2r", "eq1", "eq2", "soffr", "gqr", "gpc", "gpp",
+              "woffr", "tof", "fg", "vg", "wpc", "wps", "listr", "utr", "ons0", "ons1", "onc0", "onc1"] + \
              [k + h for k in ("pc", "pp", "hs", "qn") for h in "ab"] + ["t%s%d" % (h, b) for h in "ab" for b in range(4)]
 
 
@@ -58,7 +55,7 @@ def rank_program(g, core, T, topo):
     if rank is None:
         return
     V, P, A, Y = g.vector, g.tensor, g.scalar, g.sync
-    COPY, IDENT = ActivationFunctionType.Copy, ActivationFunctionType.Identity
+    COPY = ActivationFunctionType.Copy
     total, seen, mine = {}, {}, {}
 
     def inc(ins, name, n=1):
@@ -85,100 +82,47 @@ def rank_program(g, core, T, topo):
     def u32(v):
         return v.bitcast(dt.uint32)
 
-    def choose(out, n, even, odd, ins, add):
-        (a0, b0), (a1, b1) = even, odd
-        ne, no = (n + 1) // 2, n // 2
-        for x, v, m in ((ins[0], a0, T.me), (ins[1], b0, T.mo), (ins[2], a1, T.me), (ins[3], b1, T.mo)):
-            k = ne if x in ins[:2] else no
-            vi(V.tensor_scalar(T[x][:, 0:k], v, add, m[:, 0:1], op.add, op.mult))
-        vdep()
-        vi(V.tensor_tensor(out[:, 0:n:2], T[ins[0]][:, 0:ne], T[ins[1]][:, 0:ne], op.add))
-        vi(V.tensor_tensor(out[:, 1:n:2], T[ins[2]][:, 0:no], T[ins[3]][:, 0:no], op.add))
-        vdep()
-
     inc(Y.dma_start(T.grt[:, 0:2 * S], T.gr[:, 0:2 * S]), "ldg", 16)
     inc(A.dma_start(T.grt[:, 2 * S:4 * S], T.gr[:, 2 * S:4 * S]), "ldg", 16)
-    for k in range(8):
+    for k in range(N):
         inc((Y, A)[k % 2].dma_start(T.sni[16 * k:16 * k + 16, :], T.sn[:]), "lds", 16)
-    for k in range(8):
-        inc((Y, A)[k % 2].dma_start(T.tci[16 * k:16 * k + 16, :], T.tc[:]), "ldt", 16)
+    for k in range(N):
+        inc((Y, A)[k % 2].dma_start(T.tci[16 * k:16 * k + 16, 0:LC], T.tc[:]), "ldt", 16)
+    for k in range(N):
+        inc(Y.dma_start(T.tci[16 * k:16 * k + 16, LC:LC + 3], T.tc[:, 3 * k:3 * k + 3]), "ldt", 16)
     inc(Y.dma_start(u8(T.w2[:]), T.wc[:]), "ldw", 16)
     inc(A.dma_start(T.w2s[:], T.ws[:]), "ldw", 16)
 
-    vi(V.memset(T.zer[:], 0.0), "z")
     F32 = {"allow_small_or_imprecise_dtypes": True}
-    inc(g.iota(T.pi[:], [[1, 1]], 0, 1), "gi")
-    inc(g.iota(T.jm[:], [[16, 32]], 0, 0, **F32), "gi")
-    inc(g.iota(T.i8[:], [[CAPP, N]], -168, 0, **F32), "gi")
-    inc(g.iota(T.c48[:], [[1, CAPP]], 0, 0, **F32), "gi")
-    inc(g.iota(T.k1[:], [[0, N], [16, 3]], C + 1, 1), "gi")
+    vi(V.memset(T.zer[:], 0.0), "z")
+    inc(g.iota(T.k1[:, 0:LC + 3], [[0, N + 1], [16, 3]], C, 1), "gi")
     wait("g", g, "z")
     inc(g.affine_select(T.eb[:], T.zer[:], [[1, 516]], op.not_equal, 1.0, -3, -4), "ea")
-    vi(V.memset(T.fb[:], NONE))
-    vi(V.memset(T.vv[:, 0:16], 0.0))
-    vi(V.memset(T.vv[:, 16 + NP:416], 0.0))
+    inc(g.iota(T.vals[:], [[1, CAPP]], -MID, 3, **F32), "gi")
+    inc(g.iota(T.kf[0:32, :], [[32, BF_]], NS - MID, 1, **F32), "gi")
+    inc(g.iota(T.kv[0:32, 0:BV], [[32, BV]], 6 * NONE - MID, 1, **F32), "gi")
+    vi(V.memset(T.fb[:], float(NONE)))
+    vi(V.memset(T.r[:], 0.0))
     vi(V.memset(T.ub[:], 0.0))
-    wait("v", V, "gi")
-    vi(V.tensor_scalar(T.pm[:], T.pi[:], 4, 1, op.logical_shift_right, op.bitwise_and))
-    vi(V.tensor_scalar(T.p15i[:], T.pi[:], 15, None, op.bitwise_and))
-    vi(V.tensor_scalar(T.p4i[:], T.pi[:], 2, 3, op.logical_shift_right, op.bitwise_and))
-    vi(V.tensor_scalar(T.p3i[:], T.pi[:], 3, None, op.bitwise_and))
     vdep()
-    vi(V.tensor_copy(T.mo[:], T.pm[:]))
-    vi(V.tensor_copy(T.p15[:], T.p15i[:]))
-    vi(V.tensor_copy(T.p4[:], T.p4i[:]))
-    vi(V.tensor_copy(T.p3[:], T.p3i[:]))
-    vdep()
-    vi(V.tensor_scalar(T.sg[:], T.mo[:], 2.0, -1.0, op.mult, op.add))
-    vi(V.tensor_scalar(T.me[:], T.mo[:], -1.0, 1.0, op.mult, op.add))
-    vi(V.tensor_scalar(T.jw[:], T.jm[:], T.p15[:, 0:1], -TO, op.add, op.add))
-    vi(V.tensor_scalar(T.ew[:], T.jm[:], T.p15[:, 0:1], float(ZC), op.add, op.add))
-    vi(V.tensor_scalar(T.cm[:], T.p3[:], 2.0, None, op.min))
-    vdep()
-    vi(V.tensor_scalar(T.colv[:], T.i8[:], T.sg[:, 0:1], -24.0, op.mult, op.add), "cv")
-    vi(V.tensor_scalar(T.ca[:], T.p4[:], 3.0, T.sg[:, 0:1], op.mult, op.mult))
-    vdep()
-    vi(V.tensor_tensor(T.cb[:], T.ca[:], T.cm[:], op.add))
-    vdep()
-    vi(V.tensor_scalar(T.coff[:, 0:1], T.me[:], 21.0, T.cb[:, 0:1], op.mult, op.add))
-    vi(V.tensor_scalar(T.cd[:], T.me[:], -3.0, T.cb[:, 0:1], op.mult, op.add))
-    vdep()
-    vi(V.tensor_scalar(T.coff[:, 1:2], T.cd[:], 12.0, None, op.add))
+    vi(V.quantize_mx(T.land[:, NS:NS + ZC], T.lands[:, NS:NS + ZC], T.zer[:, 0:4 * ZC]))
     wait("a", A, "ea")
     inc(A.activation(T.e2[:], T.eb[:], COPY, scale=-0.125), "e2r")
-    wait("a", A, "cv", "gi")
-    for i in range(N):
-        inc(A.activation(T.vals[:, CAPP * i:CAPP * i + CAPP], T.c48[:], IDENT, bias=T.colv[:, i:i + 1]), "vl")
-    vi(V.quantize_mx(T.land[:, 0:ZC], T.lands[:, 0:ZC], T.zer[:, 0:4 * ZC]))
     wait("v", V, "ea")
     for b in range(4):
-        vi(V.quantize_mx(T.q1[:, 128 * b:128 * b + 128], T.q1s[:, 128 * b:128 * b + 128], T.eb[:, 3 - b:515 - b]), "eq")
-    wait("v", V, "e2r")
-    for b in range(4):
-        vi(V.quantize_mx(T.q2[:, 128 * b:128 * b + 128], T.q2s[:, 128 * b:128 * b + 128], T.e2[:, 3 - b:515 - b]), "eq")
+        vi(V.quantize_mx(T.q1[:, 128 * b:128 * b + 128], T.q1s[:, 128 * b:128 * b + 128], T.eb[:, 3 - b:515 - b]), "eq1")
 
     wait("v", V, "lds")
     vi(V.tensor_copy(T.soff[:], T.sni[:]), "soffr")
-    wait("v", V, "ldt")
-    vi(V.tensor_scalar(T.neg[:], T.tci[:], 0, None, op.is_lt))
-    vi(V.tensor_copy(T.woff[:], T.tci[:]), "woffr")
-    vdep()
-    vi(V.tensor_tensor(T.t2[:], T.neg[:], T.k1[:], op.mult))
-    vdep()
-    vi(V.tensor_tensor(T.t3[:], T.tci[:], T.t2[:], op.add))
-    vdep()
-    vi(V.tensor_copy(T.toff[:], T.t3[:]), "tof")
-    vi(V.tensor_copy(T.tord[:], T.t3[:, 0:NS // 16].indirect(T.coff[:, 0:2])))
-
     wait("v", V, "ldg")
     vi(V.quantize_mx(T.gq[:], T.gqs[:], T.grt[:]), "gqr")
     vdep()
-    vi(V.tensor_copy(u32(T.gp[:, 0:NS]), u32(T.gq[:, 0:S]).indirect(T.soff[:, 0:NS // 16])), "gpc")
+    vi(V.tensor_copy(u32(T.gp[:, 0:NS]), u32(T.gq[:, 0:S]).indirect(T.soff[:])), "gpc")
     wait("a", A, "soffr", "gqr")
-    inc(A.activation(T.gps[:, 0:NS], T.gqs[:, 0:S].indirect(T.soff[:, 0:NS // 16]), COPY), "gpp")
+    inc(A.activation(T.gps[:, 0:NS], T.gqs[:, 0:S].indirect(T.soff[:]), COPY), "gpp")
 
     dests = [(rank + k) % N for k in range(1, N)]
-    lo = ZC + CAPP * rank
+    lo = CAPP * rank
 
     def transfers(scales):
         out = []
@@ -189,7 +133,7 @@ def rank_program(g, core, T, topo):
             src = T.gps[:, a:a + CAPP] if scales else u8(T.gp[:, a:a + CAPP])
             dst = T.lands[:, lo:lo + CAPP] if scales else u8(T.land[:, lo:lo + CAPP])
             out.append(RemoteDMATransfer(dst_ids=[DstId(rid=rid, pnc=pid)], dma_engine_mask=1 << topo.engines(core, d)[k],
-                                         remote_sem=T.sem.arr, src=src, dst=dst))
+                                         remote_sem=T.sem.ars if scales else T.sem.arc, src=src, dst=dst))
         return out
 
     wait("g", g, "gpc")
@@ -197,44 +141,66 @@ def rank_program(g, core, T, topo):
     wait("g", g, "gpp")
     g.remote_dma_fused(transfers(True), local_sem=T.sem.sent)
     total["sent"] = 2 * len(dests)
-    total["arr"] = 2 * len(dests)
-    a = CAPP * rank
-    wait("y", Y, "gpc", "gpp")
-    inc(Y.dma_start(u8(T.land[:, lo:lo + CAPP]), u8(T.gp[:, a:a + CAPP])), "own", 16)
-    inc(Y.dma_start(T.lands[:, lo:lo + CAPP], T.gps[:, a:a + CAPP]), "own", 16)
+    total["arc"] = total["ars"] = len(dests)
+    wait("y", Y, "gpc")
+    inc(Y.dma_start(u8(T.land[:, lo:lo + CAPP]), u8(T.gp[:, lo:lo + CAPP])), "ownc", 16)
+    wait("y", Y, "gpp")
+    inc(Y.dma_start(T.lands[:, lo:lo + CAPP], T.gps[:, lo:lo + CAPP]), "owns", 16)
     wait("y", Y, "sent")
-    inc(Y.dma_start(u8(T.wn[:, 0:C]), T.wc[:]), "ldn", 16)
-    inc(Y.dma_start(T.wns[:, 0:C], T.ws[:]), "ldn", 16)
+    inc(Y.dma_start(u8(T.wn[:, NS:NS + C]), T.wc[:]), "ldn", 16)
+    inc(Y.dma_start(T.wns[:, NS:NS + C], T.ws[:]), "ldn", 16)
 
-    win = T.fb[:, 16:16 + FW]
-    wait("v", V, "vl")
-    for i in range(N):
-        vdep()
-        vi(V.tensor_copy(win.indirect(T.tord[:, 4 * i:4 * i + 3]), T.vals[:, CAPP * i:CAPP * i + CAPP]), "fg")
-    wait("a", A, "woffr", "ldw")
-    inc(A.activation(T.wsls[:, 0:NS], T.w2s[:, 0:C].indirect(T.woff[:, 0:NS // 16]), COPY), "wps")
+    wait("v", V, "ldt", "gi")
+    vi(V.tensor_scalar(T.t2[:, 0:LC + 3], T.tci[:, 0:LC + 3], 1023, None, op.bitwise_and))
+    vi(V.tensor_copy(T.woff[:], T.tci[:, 0:LC]), "woffr")
+    vdep()
+    vi(V.tensor_tensor(T.t3[:, 0:LC + 3], T.t2[:, 0:LC + 3], T.k1[:, 0:LC + 3], op.min))
+    vdep()
+    vi(V.tensor_copy(T.toff[:, 0:LC + 3], T.t3[:, 0:LC + 3]), "tof")
+    vdep()
+    vi(V.tensor_copy(T.fb[:, 0:FW].indirect(T.toff[:, LC:LC + 3]), T.vals[:]), "fg")
     wait("a", A, "fg", "tof")
-    inc(A.activation(T.vv[:, 16:16 + NP], win.indirect(T.toff[:, 0:NP // 16]), COPY), "vg")
+    inc(A.activation(T.vv[:], T.fb[:, 0:FW].indirect(T.toff[:, 0:NV // 16]), COPY), "vg")
+    wait("a", A, "woffr", "ldw")
+    inc(A.activation(T.wsls[:], T.w2s[:, 0:C].indirect(T.woff[:]), COPY), "wps")
+    wait("v", V, "e2r")
+    for b in range(4):
+        vi(V.quantize_mx(T.q2[:, 128 * b:128 * b + 128], T.q2s[:, 128 * b:128 * b + 128], T.e2[:, 3 - b:515 - b]), "eq2")
     wait("v", V, "ldw")
-    vi(V.tensor_copy(u32(T.wsl[:, 0:NS]), u32(T.w2[:, 0:C]).indirect(T.woff[:, 0:NS // 16])), "wpc")
+    vi(V.tensor_copy(u32(T.wsl[:]), u32(T.w2[:, 0:C]).indirect(T.woff[:])), "wpc")
+    wait("v", V, "fg")
+    vi(V.transpose(T.tt[:, 0:C], T.fb[:, 0:C]))
     wait("v", V, "vg")
+    vi(V.transpose(T.tt[:, C:C + NV], T.vv[:]))
     vdep()
-    vi(V.transpose(T.va[:], T.vv[:, 16:368]))
-    vi(V.transpose(T.vb[:], T.vv[:, 0:352]))
+    vi(V.tensor_tensor(T.ma[:], T.tt[:, 0:C:32], T.tt[:, 16:C:32], op.min))
+    vi(V.tensor_tensor(T.sa[:, 0:NB], T.tt[:, 0:C + NV:32], T.tt[:, 16:C + NV:32], op.add))
     vdep()
-    choose(T.xs, 21, (T.va[:, 16:352:32], T.vb[:, 16:352:32]), (T.vb[:, 48:352:32], T.va[:, 16:336:32]), ("x0", "x1", "x2", "x3"), MID + ZC)
-    vi(V.tensor_tensor(T.xn[:, 0:21], T.xs[:, 0:21], T.ew[:, 0:21], op.not_equal))
+    vi(V.tensor_tensor(T.mb[0:64, :], T.ma[0:64, :], T.ma[64:128, :], op.min))
     vdep()
-    vi(V.tensor_tensor(T.xm[:, 0:21], T.xs[:, 0:21], T.xn[:, 0:21], op.mult))
+    vi(V.tensor_tensor(T.sb[0:64, 0:NB], T.sa[0:64, 0:NB], T.sa[64:128, 0:NB], op.add))
     vdep()
-    vi(V.tensor_copy(T.poff[:, 0:21], T.xm[:, 0:21]), "poffr")
-    vi(V.transpose(T.fa[:], T.fb[:, 16:528]))
-    vi(V.transpose(T.fc[:], T.fb[:, 0:544]))
+    vi(V.tensor_tensor(T.mc[0:32, :], T.mb[0:32, :], T.mb[32:64, :], op.min))
     vdep()
-    choose(T.ys, 32, (T.fa[:, 0:512:32], T.fc[:, 0:512:32]), (T.fc[:, 32:544:32], T.fa[:, 0:512:32]), ("y0", "y1", "y2", "y3"), 0.0)
-    vi(V.tensor_tensor(T.ym[:], T.ys[:], T.jw[:], op.max))
+    vi(V.tensor_tensor(T.sc[0:32, 0:NB], T.sb[0:32, 0:NB], T.sb[32:64, 0:NB], op.add))
     vdep()
-    vi(V.tensor_scalar(T.foff[:], T.ym[:], TO, None, op.add), "foffr")
+    vi(V.tensor_tensor(T.dv[0:32, 0:BV], T.sc[0:32, BF_:NB], T.kv[0:32, 0:BV], op.subtract))
+    vi(V.tensor_tensor(T.r[0:32, 0:BF_], T.mc[0:32, :], T.kf[0:32, :], op.min))
+    vdep()
+    vi(V.tensor_scalar(T.r[0:32, BF_:NB], T.dv[0:32, 0:BV], float(NS - MID), None, op.min))
+    vdep()
+    vi(V.transpose(T.z[0:32, 16:48], T.r[0:32, :]))
+    vdep()
+    vi(V.tensor_copy(T.z[0:32, 0:16], T.z[0:32, 16:32]))
+    vi(V.tensor_copy(T.z[0:32, 48:64], T.z[0:32, 32:48]))
+    vdep()
+    vi(V.transpose(T.y[0:32, :], T.z[0:32, :]))
+    vdep()
+    for k in range(2):
+        vi(V.tensor_scalar(T.lst[0:32, k:2 * NB:2], T.y[0:32, 32 * k:32 * k + NB], float(MID), None, op.add), "listr")
+    vdep()
+    for q in range(1, 4):
+        vi(V.tensor_copy(T.lst[32 * q:32 * q + 32, 0:2 * NB], T.lst[0:32, 0:2 * NB]), "listr")
 
     halves = (("a", T.psa, 0, HALF, HALF), ("b", T.psb, HALF, HALF, NP - HALF))
 
@@ -242,30 +208,30 @@ def rank_program(g, core, T, topo):
         return P.matmul_mx(ps[:, 512 * b:512 * b + n], e[:, 128 * b:128 * b + 128], es[:, 128 * b:128 * b + 128],
                            x[:, at:at + n], xs[:, at:at + n], start, stop)
 
-    wait("p", P, "eq", "wpc", "wps")
+    wait("p", P, "eq1", "wpc", "wps")
     for name, ps, at, n, m in halves:
         for b in range(4):
             product(ps, b, n, T.q1, T.q1s, T.wsl, T.wsls, at, True, False)
-    wait("p", P, "arr", "own")
-    wait("v", V, "arr", "own")
-    wait("a", A, "arr", "own", "poffr")
+    wait("p", P, "eq2", "arc", "ownc", "ars", "owns")
     vdep()
+    wait("v", V, "arc", "ownc")
+    wait("a", A, "listr", "ars", "owns")
     for name, ps, at, n, m in halves:
-        off = T.poff[:, at // 16:(at + m) // 16]
-        vi(V.tensor_copy(u32(T.pk[:, at:at + m]), u32(T.land[:, 0:ZC + NS]).indirect(off)), "pc" + name)
-        inc(A.activation(T.pks[:, at:at + m], T.lands[:, 0:ZC + NS].indirect(off), COPY), "pp" + name)
+        off = T.lst[:, 2 * BF_ + at // 16:2 * BF_ + (at + m) // 16]
+        vi(V.tensor_copy(u32(T.pk[:, at:at + m]), u32(T.land[:, 0:NS + ZC]).indirect(off)), "pc" + name)
+        inc(A.activation(T.pks[:, at:at + m], T.lands[:, 0:NS + ZC].indirect(off), COPY), "pp" + name)
     for name, ps, at, n, m in halves:
         for b in range(4):
-            product(ps, b, n, T.q2, T.q2s, T.land, T.lands, ZC + at, False, False)
+            product(ps, b, n, T.q2, T.q2s, T.land, T.lands, at, False, False)
         wait("p", P, "pc" + name, "pp" + name)
         for b in range(4):
             inc(product(ps, b, m, T.q2, T.q2s, T.pk, T.pks, at, False, True), "t%s%d" % (name, b))
-    vi(V.tensor_scalar(T.u0[:], T.fa[:, 0:512:32], -MID, None, op.is_ge))
-    vi(V.tensor_tensor(T.u1[:], T.fa[:, 0:512:32], T.fa[:, 16:512:32], op.not_equal))
+    vi(V.tensor_scalar(T.u0[0:32, :], T.sc[0:32, 0:BF_], 7.5 * NONE, None, op.is_lt))
+    vi(V.tensor_scalar(T.u1[0:32, :], T.sc[0:32, 0:BF_], 6.625 * NONE, None, op.is_lt))
     vdep()
-    vi(V.tensor_tensor(T.ub[:, 0:16], T.u0[:], T.u1[:], op.add))
+    vi(V.tensor_tensor(T.ub[0:32, 0:BF_], T.u0[0:32, :], T.u1[0:32, :], op.add))
     vdep()
-    vi(V.transpose(T.ut[:], T.ub[:]), "utr")
+    vi(V.transpose(T.ut[0:32, :], T.ub[0:32, :]), "utr")
 
     for name, ps, at, n, m in halves:
         for b in range(4):
@@ -278,15 +244,15 @@ def rank_program(g, core, T, topo):
                 inc(A.activation(out, src, COPY), "hs" + name)
         wait("v", V, "hs" + name)
         vdep()
-        vi(V.quantize_mx(T.wn[:, C + at:C + at + n], T.wns[:, C + at:C + at + n], T.h[:, 4 * at:4 * (at + n)]), "qn" + name)
+        vi(V.quantize_mx(T.wn[:, at:at + n], T.wns[:, at:at + n], T.h[:, 4 * at:4 * (at + n)]), "qn" + name)
 
     wait("v", V, "ldn")
     vdep()
-    wait("a", A, "ldn", "qna", "qnb", "foffr")
+    wait("a", A, "ldn", "qna", "qnb")
     for k in range(2):
-        off = T.foff[:, 16 * k:16 * k + 16]
-        vi(V.tensor_copy(u32(T.on[:, 256 * k:256 * k + 256]), u32(T.wn[:, 0:C + NS]).indirect(off)), "onc%d" % k)
-        inc(A.activation(T.ons[:, 256 * k:256 * k + 256], T.wns[:, 0:C + NS].indirect(off), COPY), "ons%d" % k)
+        off = T.lst[:, 16 * k:16 * k + 16]
+        vi(V.tensor_copy(u32(T.on[:, 256 * k:256 * k + 256]), u32(T.wn[:, 0:NS + C]).indirect(off)), "onc%d" % k)
+        inc(A.activation(T.ons[:, 256 * k:256 * k + 256], T.wns[:, 0:NS + C].indirect(off), COPY), "ons%d" % k)
     wait("y", Y, "utr")
     inc(Y.dma_start(T.up[:], T.ut[0:16, :]), "st", 16)
     for k in range(2):

from concourse.bass import DstId, RemoteDMATransfer
from concourse.mybir import dt, AluOpType as op, ActivationFunctionType

X4, U8 = "float8_e4m3fn_x4", "uint8"
C, S, CAPP, N = 512, 256, 48, 8
NS = N * CAPP
HALF = NS // 2
ZC = 128
NP = NS - CAPP
NV = 352
FW = C + 160
MID, NONE = 192, 768
LC = NS // 16
BF_, BV = C // 32, NV // 32
NB = BF_ + BV

SCRATCH = {
    "grt": ("sbuf", [128, 4 * S], "bfloat16"),
    "sni": ("sbuf", [128, LC], "int32"), "tci": ("sbuf", [128, 28], "int32"),
    "soff": ("sbuf", [128, LC], "uint16"), "woff": ("sbuf", [128, LC], "uint16"),
    "gq": ("sbuf", [128, S], X4), "gqs": ("sbuf", [128, S], U8),
    "gp": ("sbuf", [128, NS], X4), "gps": ("sbuf", [128, NS], U8),
    "land": ("sbuf", [128, NS + ZC], X4), "lands": ("sbuf", [128, NS + ZC], U8),
    "w2": ("sbuf", [128, C], X4), "w2s": ("sbuf", [128, C], U8),
    "wsl": ("sbuf", [128, NS], X4), "wsls": ("sbuf", [128, NS], U8),
    "pk": ("sbuf", [128, NS], X4), "pks": ("sbuf", [128, NS], U8),
    "wn": ("sbuf", [128, NS + C], X4), "wns": ("sbuf", [128, NS + C], U8),
    "on": ("sbuf", [128, C], X4), "ons": ("sbuf", [128, C], U8),
    "zer": ("sbuf", [128, 516], "bfloat16"), "eb": ("sbuf", [128, 516], "bfloat16"), "e2": ("sbuf", [128, 516], "bfloat16"),
    "q1": ("sbuf", [128, 512], X4), "q1s": ("sbuf", [128, 512], U8),
    "q2": ("sbuf", [128, 512], X4), "q2s": ("sbuf", [128, 512], U8),
    "k1": ("sbuf", [128, 28], "int32"), "t2": ("sbuf", [128, 28], "int32"), "t3": ("sbuf", [128, 28], "int32"),
    "toff": ("sbuf", [128, 28], "uint16"),
    "vals": ("sbuf", [128, CAPP], "bfloat16"),
    "fb": ("sbuf", [128, FW], "bfloat16"),
    "vv": ("sbuf", [128, NV], "bfloat16"),
    "tt": ("sbuf", [128, C + NV], "bfloat16"),
    "sa": ("sbuf", [128, 32], "float32"), "sb": ("sbuf", [128, 32], "float32"), "sc": ("sbuf", [128, 32], "float32"),
    "ma": ("sbuf", [128, 16], "float32"), "mb": ("sbuf", [128, 16], "float32"), "mc": ("sbuf", [128, 16], "float32"),
    "kf": ("sbuf", [128, 16], "float32"), "kv": ("sbuf", [128, 16], "float32"), "dv": ("sbuf", [128, 16], "float32"),
    "r": ("sbuf", [128, 32], "float32"), "z": ("sbuf", [128, 64], "float32"), "y": ("sbuf", [128, 64], "float32"),
    "lst": ("sbuf", [128, 64], "uint16"),
    "u0": ("sbuf", [128, 16], "float32"), "u1": ("sbuf", [128, 16], "float32"),
    "ub": ("sbuf", [128, 32], "float32"), "ut": ("sbuf", [128, 32], "float32"),
    "h": ("sbuf", [128, 4 * NS], "bfloat16"),
    "psa": ("psum", [128, 2048], "float32"), "psb": ("psum", [128, 2048], "float32"),
}
SEMAPHORES = ["ldg", "lds", "ldt", "ldw", "ldn", "ownc", "owns", "st", "arc", "ars", "sent", "v", "z", "gi", "ea", "e2r", "eq1", "eq2", "soffr", "gqr", "gpc", "gpp",
              "woffr", "tof", "fg", "vg", "wpc", "wps", "listr", "utr", "ons0", "ons1", "onc0", "onc1"] + \
             [k + h for k in ("pc", "pp", "hs", "qn") for h in "ab"] + ["t%s%d" % (h, b) for h in "ab" for b in range(4)]


def rank_program(g, core, T, topo):
    rank = T.rank_of(core)
    if rank is None:
        return
    V, P, A, Y = g.vector, g.tensor, g.scalar, g.sync
    COPY = ActivationFunctionType.Copy
    total, seen, mine = {}, {}, {}

    def inc(ins, name, n=1):
        ins.then_inc(T.sem[name], n)
        total[name] = total.get(name, 0) + n
        return name

    def wait(qn, q, *evs):
        for name in evs:
            if seen.get((qn, name), 0) < total[name]:
                q.wait_ge(T.sem[name], total[name])
                seen[(qn, name)] = total[name]

    def vi(ins, name="v"):
        mine[inc(ins, name)] = 1

    def vdep():
        wait("v", V, *sorted(mine))
        mine.clear()

    def u8(v):
        return v.bitcast(dt.uint8)

    def u32(v):
        return v.bitcast(dt.uint32)

    inc(Y.dma_start(T.grt[:, 0:2 * S], T.gr[:, 0:2 * S]), "ldg", 16)
    inc(A.dma_start(T.grt[:, 2 * S:4 * S], T.gr[:, 2 * S:4 * S]), "ldg", 16)
    for k in range(N):
        inc((Y, A)[k % 2].dma_start(T.sni[16 * k:16 * k + 16, :], T.sn[:]), "lds", 16)
    for k in range(N):
        inc((Y, A)[k % 2].dma_start(T.tci[16 * k:16 * k + 16, 0:LC], T.tc[:]), "ldt", 16)
    for k in range(N):
        inc(Y.dma_start(T.tci[16 * k:16 * k + 16, LC:LC + 3], T.tc[:, 3 * k:3 * k + 3]), "ldt", 16)
    inc(Y.dma_start(u8(T.w2[:]), T.wc[:]), "ldw", 16)
    inc(A.dma_start(T.w2s[:], T.ws[:]), "ldw", 16)

    F32 = {"allow_small_or_imprecise_dtypes": True}
    vi(V.memset(T.zer[:], 0.0), "z")
    inc(g.iota(T.k1[:, 0:LC + 3], [[0, N + 1], [16, 3]], C, 1), "gi")
    wait("g", g, "z")
    inc(g.affine_select(T.eb[:], T.zer[:], [[1, 516]], op.not_equal, 1.0, -3, -4), "ea")
    inc(g.iota(T.vals[:], [[1, CAPP]], -MID, 3, **F32), "gi")
    inc(g.iota(T.kf[0:32, :], [[32, BF_]], NS - MID, 1, **F32), "gi")
    inc(g.iota(T.kv[0:32, 0:BV], [[32, BV]], 6 * NONE - MID, 1, **F32), "gi")
    vi(V.memset(T.fb[:], float(NONE)))
    vi(V.memset(T.r[:], 0.0))
    vi(V.memset(T.ub[:], 0.0))
    vdep()
    vi(V.quantize_mx(T.land[:, NS:NS + ZC], T.lands[:, NS:NS + ZC], T.zer[:, 0:4 * ZC]))
    wait("a", A, "ea")
    inc(A.activation(T.e2[:], T.eb[:], COPY, scale=-0.125), "e2r")
    wait("v", V, "ea")
    for b in range(4):
        vi(V.quantize_mx(T.q1[:, 128 * b:128 * b + 128], T.q1s[:, 128 * b:128 * b + 128], T.eb[:, 3 - b:515 - b]), "eq1")

    wait("v", V, "lds")
    vi(V.tensor_copy(T.soff[:], T.sni[:]), "soffr")
    wait("v", V, "ldg")
    vi(V.quantize_mx(T.gq[:], T.gqs[:], T.grt[:]), "gqr")
    vdep()
    vi(V.tensor_copy(u32(T.gp[:, 0:NS]), u32(T.gq[:, 0:S]).indirect(T.soff[:])), "gpc")
    wait("a", A, "soffr", "gqr")
    inc(A.activation(T.gps[:, 0:NS], T.gqs[:, 0:S].indirect(T.soff[:]), COPY), "gpp")

    dests = [(rank + k) % N for k in range(1, N)]
    lo = CAPP * rank

    def transfers(scales):
        out = []
        for k, q in enumerate(dests):
            d = T.cores[q]
            rid, pid = topo.addr(d, core)
            a = CAPP * q
            src = T.gps[:, a:a + CAPP] if scales else u8(T.gp[:, a:a + CAPP])
            dst = T.lands[:, lo:lo + CAPP] if scales else u8(T.land[:, lo:lo + CAPP])
            out.append(RemoteDMATransfer(dst_ids=[DstId(rid=rid, pnc=pid)], dma_engine_mask=1 << topo.engines(core, d)[k],
                                         remote_sem=T.sem.ars if scales else T.sem.arc, src=src, dst=dst))
        return out

    wait("g", g, "gpc")
    g.remote_dma_fused(transfers(False), local_sem=T.sem.sent)
    wait("g", g, "gpp")
    g.remote_dma_fused(transfers(True), local_sem=T.sem.sent)
    total["sent"] = 2 * len(dests)
    total["arc"] = total["ars"] = len(dests)
    wait("y", Y, "gpc")
    inc(Y.dma_start(u8(T.land[:, lo:lo + CAPP]), u8(T.gp[:, lo:lo + CAPP])), "ownc", 16)
    wait("y", Y, "gpp")
    inc(Y.dma_start(T.lands[:, lo:lo + CAPP], T.gps[:, lo:lo + CAPP]), "owns", 16)
    wait("y", Y, "sent")
    inc(Y.dma_start(u8(T.wn[:, NS:NS + C]), T.wc[:]), "ldn", 16)
    inc(Y.dma_start(T.wns[:, NS:NS + C], T.ws[:]), "ldn", 16)

    wait("v", V, "ldt", "gi")
    vi(V.tensor_scalar(T.t2[:, 0:LC + 3], T.tci[:, 0:LC + 3], 1023, None, op.bitwise_and))
    vi(V.tensor_copy(T.woff[:], T.tci[:, 0:LC]), "woffr")
    vdep()
    vi(V.tensor_tensor(T.t3[:, 0:LC + 3], T.t2[:, 0:LC + 3], T.k1[:, 0:LC + 3], op.min))
    vdep()
    vi(V.tensor_copy(T.toff[:, 0:LC + 3], T.t3[:, 0:LC + 3]), "tof")
    vdep()
    vi(V.tensor_copy(T.fb[:, 0:FW].indirect(T.toff[:, LC:LC + 3]), T.vals[:]), "fg")
    wait("a", A, "fg", "tof")
    inc(A.activation(T.vv[:], T.fb[:, 0:FW].indirect(T.toff[:, 0:NV // 16]), COPY), "vg")
    wait("a", A, "woffr", "ldw")
    inc(A.activation(T.wsls[:], T.w2s[:, 0:C].indirect(T.woff[:]), COPY), "wps")
    wait("v", V, "e2r")
    for b in range(4):
        vi(V.quantize_mx(T.q2[:, 128 * b:128 * b + 128], T.q2s[:, 128 * b:128 * b + 128], T.e2[:, 3 - b:515 - b]), "eq2")
    wait("v", V, "ldw")
    vi(V.tensor_copy(u32(T.wsl[:]), u32(T.w2[:, 0:C]).indirect(T.woff[:])), "wpc")
    wait("v", V, "fg")
    vi(V.transpose(T.tt[:, 0:C], T.fb[:, 0:C]))
    wait("v", V, "vg")
    vi(V.transpose(T.tt[:, C:C + NV], T.vv[:]))
    vdep()
    vi(V.tensor_tensor(T.ma[:], T.tt[:, 0:C:32], T.tt[:, 16:C:32], op.min))
    vi(V.tensor_tensor(T.sa[:, 0:NB], T.tt[:, 0:C + NV:32], T.tt[:, 16:C + NV:32], op.add))
    vdep()
    vi(V.tensor_tensor(T.mb[0:64, :], T.ma[0:64, :], T.ma[64:128, :], op.min))
    vdep()
    vi(V.tensor_tensor(T.sb[0:64, 0:NB], T.sa[0:64, 0:NB], T.sa[64:128, 0:NB], op.add))
    vdep()
    vi(V.tensor_tensor(T.mc[0:32, :], T.mb[0:32, :], T.mb[32:64, :], op.min))
    vdep()
    vi(V.tensor_tensor(T.sc[0:32, 0:NB], T.sb[0:32, 0:NB], T.sb[32:64, 0:NB], op.add))
    vdep()
    vi(V.tensor_tensor(T.dv[0:32, 0:BV], T.sc[0:32, BF_:NB], T.kv[0:32, 0:BV], op.subtract))
    vi(V.tensor_tensor(T.r[0:32, 0:BF_], T.mc[0:32, :], T.kf[0:32, :], op.min))
    vdep()
    vi(V.tensor_scalar(T.r[0:32, BF_:NB], T.dv[0:32, 0:BV], float(NS - MID), None, op.min))
    vdep()
    vi(V.transpose(T.z[0:32, 16:48], T.r[0:32, :]))
    vdep()
    vi(V.tensor_copy(T.z[0:32, 0:16], T.z[0:32, 16:32]))
    vi(V.tensor_copy(T.z[0:32, 48:64], T.z[0:32, 32:48]))
    vdep()
    vi(V.transpose(T.y[0:32, :], T.z[0:32, :]))
    vdep()
    for k in range(2):
        vi(V.tensor_scalar(T.lst[0:32, k:2 * NB:2], T.y[0:32, 32 * k:32 * k + NB], float(MID), None, op.add), "listr")
    vdep()
    for q in range(1, 4):
        vi(V.tensor_copy(T.lst[32 * q:32 * q + 32, 0:2 * NB], T.lst[0:32, 0:2 * NB]), "listr")

    halves = (("a", T.psa, 0, HALF, HALF), ("b", T.psb, HALF, HALF, NP - HALF))

    def product(ps, b, n, e, es, x, xs, at, start, stop):
        return P.matmul_mx(ps[:, 512 * b:512 * b + n], e[:, 128 * b:128 * b + 128], es[:, 128 * b:128 * b + 128],
                           x[:, at:at + n], xs[:, at:at + n], start, stop)

    wait("p", P, "eq1", "wpc", "wps")
    for name, ps, at, n, m in halves:
        for b in range(4):
            product(ps, b, n, T.q1, T.q1s, T.wsl, T.wsls, at, True, False)
    wait("p", P, "eq2", "arc", "ownc", "ars", "owns")
    vdep()
    wait("v", V, "arc", "ownc")
    wait("a", A, "listr", "ars", "owns")
    for name, ps, at, n, m in halves:
        off = T.lst[:, 2 * BF_ + at // 16:2 * BF_ + (at + m) // 16]
        vi(V.tensor_copy(u32(T.pk[:, at:at + m]), u32(T.land[:, 0:NS + ZC]).indirect(off)), "pc" + name)
        inc(A.activation(T.pks[:, at:at + m], T.lands[:, 0:NS + ZC].indirect(off), COPY), "pp" + name)
    for name, ps, at, n, m in halves:
        for b in range(4):
            product(ps, b, n, T.q2, T.q2s, T.land, T.lands, at, False, False)
        wait("p", P, "pc" + name, "pp" + name)
        for b in range(4):
            inc(product(ps, b, m, T.q2, T.q2s, T.pk, T.pks, at, False, True), "t%s%d" % (name, b))
    vi(V.tensor_scalar(T.u0[0:32, :], T.sc[0:32, 0:BF_], 7.5 * NONE, None, op.is_lt))
    vi(V.tensor_scalar(T.u1[0:32, :], T.sc[0:32, 0:BF_], 6.625 * NONE, None, op.is_lt))
    vdep()
    vi(V.tensor_tensor(T.ub[0:32, 0:BF_], T.u0[0:32, :], T.u1[0:32, :], op.add))
    vdep()
    vi(V.transpose(T.ut[0:32, :], T.ub[0:32, :]), "utr")

    for name, ps, at, n, m in halves:
        for b in range(4):
            out, src = T.h[:, 4 * at + b:4 * (at + n):4], ps[:, 512 * b:512 * b + n]
            if b % 2 == 0:
                wait("v", V, "t%s%d" % (name, b))
                vi(V.tensor_copy(out, src))
            else:
                wait("a", A, "t%s%d" % (name, b))
                inc(A.activation(out, src, COPY), "hs" + name)
        wait("v", V, "hs" + name)
        vdep()
        vi(V.quantize_mx(T.wn[:, at:at + n], T.wns[:, at:at + n], T.h[:, 4 * at:4 * (at + n)]), "qn" + name)

    wait("v", V, "ldn")
    vdep()
    wait("a", A, "ldn", "qna", "qnb")
    for k in range(2):
        off = T.lst[:, 16 * k:16 * k + 16]
        vi(V.tensor_copy(u32(T.on[:, 256 * k:256 * k + 256]), u32(T.wn[:, 0:NS + C]).indirect(off)), "onc%d" % k)
        inc(A.activation(T.ons[:, 256 * k:256 * k + 256], T.wns[:, 0:NS + C].indirect(off), COPY), "ons%d" % k)
    wait("y", Y, "utr")
    inc(Y.dma_start(T.up[:], T.ut[0:16, :]), "st", 16)
    for k in range(2):
        wait("y", Y, "onc%d" % k)
        inc(Y.dma_start(T.oc[:, 1024 * k:1024 * k + 1024], u8(T.on[:, 256 * k:256 * k + 256])), "st", 16)
    for k in range(4):
        qn, q = (("a", A), ("y", Y))[k // 2]
        wait(qn, q, "ons0", "ons1")
        inc(q.dma_start(T.osc[4 * k:4 * k + 4, :], T.ons[32 * k:32 * k + 4, :]), "st", 16)

    for name in total:
        if name not in ("st",):
            wait("g", g, name)
    wait("y", Y, "st")
